import numpy as np
import ml_dtypes


def mxq(x, axis, fmt="e4m3"):
    dtype, down = {"e4m3": (ml_dtypes.float8_e4m3fn, 7), "e5m2": (ml_dtypes.float8_e5m2, 14)}[fmt]
    v = np.moveaxis(np.asarray(x, np.float32).astype(ml_dtypes.bfloat16).astype(np.float64), axis, -1)
    blocks = v.reshape(v.shape[:-1] + (-1, 32))
    amax = np.abs(blocks).max(-1, keepdims=True)
    byte = np.maximum(np.where(amax > 0, np.frexp(amax)[1] - 1 + 127, 0) - down, 1)
    scale = np.exp2(byte - 127.0)
    codes = (blocks / scale).astype(np.float32).astype(dtype).astype(np.float64)
    return np.moveaxis((codes * scale).reshape(v.shape), -1, axis)


WIDE = False


def mx_kscale(k):
    if not WIDE:
        return np.ones(k)
    levels = np.array([10, -10, 5, -5, 0])
    if k % 512:
        return np.exp2(np.random.permutation(np.resize(levels, k // 32))).repeat(32)
    a = np.empty((k // 512, 16))
    for p in range(k // 512):
        a[p, :8] = np.random.permutation(np.resize(levels, 8))
        for g in range(8):
            far = levels[np.abs(levels - a[p, g]) >= 10]
            a[p, g + 8] = far[np.random.randint(len(far))]
    return np.exp2(a.ravel()).repeat(32)


def f64(x):
    return np.asarray(x).astype(np.float64)


def striped(idx):
    return np.tile(np.asarray(idx).reshape(-1, 16).T, (8, 1)).astype(np.uint16)


def unstriped(offs):
    return offs[:16].T.reshape(-1).astype(np.int64)


def striped8(idx):
    return np.asarray(idx).reshape(8, -1, 16).transpose(0, 2, 1).reshape(128, -1).astype(np.uint16)


def unstriped8(offs):
    return offs.reshape(8, 16, -1).transpose(0, 2, 1).reshape(8, -1).astype(np.int64)


def pick8(x, idx, run):
    r = np.arange(len(x))
    return x[r[:, None], idx[r % (8 * run) // run]]


E2M1 = np.array([0.0, 0.5, 1.0, 1.5, 2.0, 3.0, 4.0, 6.0, -0.0, -0.5, -1.0, -1.5, -2.0, -3.0, -4.0, -6.0])


def pack_weight(w, fmt):
    k, n = w.shape
    w = f64(np.asarray(w, np.float32).astype(ml_dtypes.bfloat16)).reshape(k // 32, 32, n)
    amax = np.abs(w).max(1)
    if fmt == "e4m3":
        byte = np.frexp(amax)[1] - 1 + 127 - 7
    else:
        mant, ex = np.frexp(amax / 6.0)
        byte = np.where(mant > 0.5, ex, ex - 1) + 127
    byte = np.clip(np.where(amax > 0, byte, 1), 1, 254)
    scaled = (w * np.exp2(127.0 - byte)[:, None, :]).reshape(k, n).astype(np.float32)
    by_word = np.ascontiguousarray(scaled.reshape(k // 512, 128, 4, n).transpose(0, 1, 3, 2))
    if fmt == "e4m3":
        words = by_word.astype(ml_dtypes.float8_e4m3fn).view(np.uint8)
    else:
        c = by_word.astype(ml_dtypes.float4_e2m1fn).view(np.uint8) & 0xF
        words = (c[..., 0::2] | (c[..., 1::2] << 4)).reshape(k // 512, 128, 2 * n)
    return np.ascontiguousarray(words), np.ascontiguousarray(byte.astype(np.uint8).reshape(k // 512, 16, n))


def unpack_weight(words, scales, fmt):
    g, _, n = scales.shape
    words = np.ascontiguousarray(words).reshape(g, 128, n, -1)
    if fmt == "e4m3":
        vals = words.view(ml_dtypes.float8_e4m3fn).astype(np.float64)
    else:
        nib = np.empty((g, 128, n, 4), np.uint8)
        nib[..., 0::2] = words & 0xF
        nib[..., 1::2] = words >> 4
        vals = E2M1[nib]
    vals = vals * np.repeat(np.exp2(scales.astype(np.float64) - 127.0), 8, axis=1)[..., None]
    return vals.transpose(0, 1, 3, 2).reshape(g * 512, n)


K, J, R, T, U, C, O, S, N, Z = 512, 256, 512, 512, 512, 512, 128, 256, 256, 1024


def setup_inputs():
    n = np.random.standard_normal
    idx = np.stack([np.random.permutation(T)[:J] for _ in range(8)])
    idx2 = np.stack([np.random.permutation(U)[:J] for _ in range(8)])
    idx3 = np.stack([np.random.permutation(C)[:J] for _ in range(8)])
    idx4 = np.stack([np.random.permutation(C)[:S] for _ in range(8)])
    idx5 = np.random.permutation(C)[:S]
    idx6 = np.stack([np.random.permutation(S)[:O] for _ in range(8)])
    idx7 = np.random.permutation(Z)[:N]
    fk = mx_kscale(K)
    fr = mx_kscale(R)
    wp = pack_weight(n((K, R)) * 1 / np.sqrt(K) / fk[:, None] * fr, "e4m3")
    vsp = pack_weight(n((R, Z)) * 1 / np.sqrt(R) / fr[:, None], "e2m1")
    return {
        "ta": (np.random.randint(-7, 8, (K, T)).astype(np.float64)).astype(np.float32),
        "tb": (np.random.randint(-7, 8, (K, U)).astype(np.float64)).astype(np.float32),
        "ga": ((np.random.randint(8, 25, (K, 1)) / 64.0) * fk[:, None]).astype(np.float32),
        "gb": ((np.random.randint(8, 25, (K, 1)) / 64.0) * fk[:, None]).astype(np.float32),
        "w_words": wp[0],
        "w_scales": wp[1],
        "sa": (np.random.uniform(0.5, 1.6, (R, 1))).astype(np.float32),
        "sb": (np.random.uniform(0.5, 1.6, (R, 1))).astype(np.float32),
        "sd": (np.random.uniform(0.5, 1.6, (R, 1))).astype(np.float32),
        "vs_words": vsp[0],
        "vs_scales": vsp[1],
        "offs": striped8(idx),
        "offs2": striped8(idx2),
        "offs3": striped8(idx3),
        "offs4": striped8(idx4),
        "offs5": striped(idx5),
        "offs6": striped8(idx6),
        "offs7": striped(idx7),
    }


def reference(ta, tb, ga, gb, w_words, w_scales, sa, sb, sd, vs_words, vs_scales, offs, offs2, offs3, offs4, offs5, offs6, offs7):
    idx = unstriped8(offs)
    idx2 = unstriped8(offs2)
    idx3 = unstriped8(offs3)
    idx4 = unstriped8(offs4)
    idx5 = unstriped(offs5)
    idx6 = unstriped8(offs6)
    idx7 = unstriped(offs7)
    wu = unpack_weight(w_words, w_scales, "e4m3")
    vsu = unpack_weight(vs_words, vs_scales, "e2m1")
    xc = np.maximum(pick8(f64(ta), idx, 64) * f64(ga), pick8(f64(tb), idx2, 64) * f64(gb))
    xcq = mxq(xc, 0, "e4m3")
    a = wu.T @ xcq
    pw = np.zeros((R, C))
    pw[np.arange(R)[:, None], idx3[np.arange(R) % 512 // 64]] = a
    pg = np.maximum(pick8(pw, idx4, 64) * f64(sa), pw[:, idx5] * f64(sb))
    hid = pick8(pg, idx6, 64) * f64(sd)
    vsidx7g = vsu[:, idx7]
    hidq = mxq(hid, 0, "e4m3")
    y = vsidx7g.T @ hidq
    return y

@@ -1,0 +1,195 @@
+from contextlib import ExitStack
+
+import concourse.mybir as mybir
+
+K, J, R, T, U, C, O, S, N, Z = 512, 256, 512, 512, 512, 512, 128, 256, 256, 1024
+FLOPS = 2 * K * R * J + 2 * R * N * O
+
+F32 = mybir.dt.float32
+BF16 = mybir.dt.bfloat16
+I32 = mybir.dt.int32
+U32 = mybir.dt.uint32
+U16 = mybir.dt.uint16
+U8 = mybir.dt.uint8
+FP8X4 = mybir.dt.float8_e4m3fn_x4
+FP4X4 = mybir.dt.float4_e2m1fn_x4
+COPY = mybir.ActivationFunctionType.Copy
+MAX = mybir.AluOpType.max
+
+P = 128
+PACK = 4
+HALF = J // 2
+
+
+def tile_picked_largercode_plain_one_ladder_store_plain_kernel(
+    tc, ta, tb, ga, gb, w_words, w_scales, sa, sb, sd, vs_words, vs_scales,
+    offs, offs2, offs3, offs4, offs5, offs6, offs7, out,
+):
+    nc = tc.nc
+    with ExitStack() as ctx:
+        keep = ctx.enter_context(tc.tile_pool(name="keep", bufs=1))
+        psum = ctx.enter_context(tc.psum_pool(name="psum", bufs=1))
+
+        def sbuf(name, shape, dtype):
+            return keep.tile(shape, dtype, name=name, align_bytes=64)
+
+        def load_list(name, src):
+            t = sbuf(name, list(src.shape), U16)
+            nc.sync.dma_start(t[:], src)
+            return t
+
+        def load_factor(queue, name, src):
+            t = sbuf(name, [P, PACK], F32)
+            queue.dma_start(t[:], src.rearrange("(p t) o -> p (t o)", t=PACK))
+            return t
+
+        def load_rows(name, src, t):
+            rows = sbuf(name, [P, src.shape[1]], F32)
+            nc.sync.dma_start(rows[:], src.rearrange("(p t) c -> p t c", t=PACK)[:, t, :])
+            return rows
+
+        def stage_scales(name, src):
+            width = src.shape[2]
+            staged = sbuf(name, [4, 4, width // 4], I32)
+            nc.gpsimd.dma_start(staged[:], src[0].rearrange("(q i) c -> i q c", i=4).bitcast(I32))
+            return staged
+
+        def spread_scales(name, staged):
+            words = staged.shape[2]
+            plane = sbuf(name, [P, 4 * words], U8)
+            nc.vector.memset(plane[:].bitcast(I32), 0)
+            for q in range(4):
+                nc.vector.tensor_copy(plane[32 * q : 32 * q + 4, :].bitcast(I32), staged[:, q, :])
+            return plane
+
+        l1 = load_list("l1", offs)
+        ta_rows = [load_rows("ta0", ta, 0)]
+        ga_t = load_factor(nc.scalar, "ga_t", ga)
+        gb_t = load_factor(nc.scalar, "gb_t", gb)
+        l2 = load_list("l2", offs2)
+        tb_rows = [load_rows("tb0", tb, 0)]
+        ta_rows.append(load_rows("ta1", ta, 1))
+        tb_rows.append(load_rows("tb1", tb, 1))
+        l7 = load_list("l7", offs7)
+        for t in range(2, PACK):
+            ta_rows.append(load_rows("ta%d" % t, ta, t))
+            tb_rows.append(load_rows("tb%d" % t, tb, t))
+        w_raw = sbuf("w_raw", [P, R], U32)
+        nc.sync.dma_start(w_raw[:].bitcast(I32), w_words[0].rearrange("p n t -> p (n t)").bitcast(I32))
+        l3 = load_list("l3", offs3)
+        l4 = load_list("l4", offs4)
+        l5 = load_list("l5", offs5)
+        sa_t = load_factor(nc.sync, "sa_t", sa)
+        sb_t = load_factor(nc.sync, "sb_t", sb)
+        vs_raw = sbuf("vs_raw", [P, Z], U16)
+        nc.sync.dma_start(vs_raw[:].bitcast(I32), vs_words[0].bitcast(I32))
+        l6 = load_list("l6", offs6)
+        sd_t = load_factor(nc.sync, "sd_t", sd)
+        ws_staged = stage_scales("ws_staged", w_scales)
+        vss_staged = stage_scales("vss_staged", vs_scales)
+
+        board = [sbuf("board%d" % t, [P, C], F32) for t in range(PACK)]
+        for t in range(PACK):
+            nc.vector.memset(board[t][:], 0.0)
+        ws_plain = spread_scales("ws_plain", ws_staged)
+        ws_dealt = sbuf("ws_dealt", [P, R], U8)
+        nc.vector.tensor_copy(
+            ws_dealt[:].rearrange("p (t m) -> p m t", t=PACK), ws_plain[:].rearrange("p (m t) -> p m t", t=PACK)
+        )
+        vss_plain = spread_scales("vss_plain", vss_staged)
+        vss_picked = sbuf("vss_picked", [P, N], U8)
+        nc.vector.tensor_copy(vss_picked[:], vss_plain[:].indirect(l7[:]))
+
+        xc = [sbuf("xc%d" % h, [P, HALF, PACK], BF16) for h in range(2)]
+        xq = sbuf("xq", [P, J], U32)
+        xs = sbuf("xs", [P, J], U8)
+        halves = [slice(h * HALF, (h + 1) * HALF) for h in range(2)]
+        cols = [slice(h * HALF // 16, (h + 1) * HALF // 16) for h in range(2)]
+        for t in range(PACK):
+            pa = sbuf("pa%d" % t, [P, J], F32)
+            pb = [sbuf("pb%d_%d" % (t, h), [P, HALF], F32) for h in range(2)] if t == PACK - 1 else None
+            nc.scalar.activation(pa[:], ta_rows[t][:].indirect(l1[:]), COPY, scale=ga_t[:, t : t + 1])
+            if t < PACK - 1:
+                pbw = sbuf("pb%d" % t, [P, J], F32)
+                nc.scalar.activation(pbw[:], tb_rows[t][:].indirect(l2[:]), COPY, scale=gb_t[:, t : t + 1])
+                for h in range(2):
+                    nc.vector.tensor_tensor(xc[h][:, :, t], pa[:, halves[h]], pbw[:, halves[h]], MAX)
+            else:
+                for h in range(2):
+                    nc.scalar.activation(pb[h][:], tb_rows[t][:].indirect(l2[:, cols[h]]), COPY, scale=gb_t[:, t : t + 1])
+                for h in range(2):
+                    nc.vector.tensor_tensor(xc[h][:, :, t], pa[:, halves[h]], pb[h][:], MAX)
+        for h in range(2):
+            nc.vector.quantize_mx(
+                out=xq[:, halves[h]].bitcast(FP8X4), scales=xs[:, halves[h]], in_=xc[h][:].rearrange("p j t -> p (j t)")
+            )
+
+        w_dealt = sbuf("w_dealt", [P, R], U32)
+        nc.scalar.copy(
+            w_dealt[:].rearrange("p (t m) -> p m t", t=PACK), w_raw[:].rearrange("p (m t) -> p m t", t=PACK)
+        )
+
+        def first_product(name, t, js):
+            n = js.stop - js.start
+            acc = psum.tile([P, n], F32, name="acc_" + name)
+            nc.tensor.matmul_mx(
+                acc[:], lhsT=w_dealt[:, t * P : (t + 1) * P].bitcast(FP8X4), lhsT_scale=ws_dealt[:, t * P : (t + 1) * P],
+                rhs=xq[:, js].bitcast(FP8X4), rhs_scale=xs[:, js], start=True, stop=True,
+            )
+            a = sbuf("a_" + name, [P, n], F32)
+            nc.scalar.copy(a[:], acc[:])
+            return a
+
+        a0 = [first_product("0_%d" % h, 0, halves[h]) for h in range(2)]
+        a_rest = [first_product("%d" % t, t, slice(0, J)) for t in range(1, PACK)]
+
+        hid = sbuf("hid", [P, PACK, O], BF16)
+
+        def scatter(t):
+            if t == 0:
+                for h in range(2):
+                    nc.vector.tensor_copy(board[0][:].indirect(l3[:, cols[h]]), a0[h][:])
+            else:
+                nc.vector.tensor_copy(board[t][:].indirect(l3[:]), a_rest[t - 1][:])
+
+        def fetch_stops(t):
+            own = sbuf("own%d" % t, [P, S], F32)
+            shared = sbuf("shared%d" % t, [P, S], F32)
+            nc.scalar.activation(own[:], board[t][:].indirect(l4[:]), COPY, scale=sa_t[:, t : t + 1])
+            nc.scalar.activation(shared[:], board[t][:].indirect(l5[:]), COPY, scale=sb_t[:, t : t + 1])
+            return own, shared
+
+        def keep_larger(t, pair):
+            pg = sbuf("pg%d" % t, [P, S], F32)
+            nc.vector.tensor_tensor(pg[:], pair[0][:], pair[1][:], MAX)
+            nc.scalar.activation(hid[:, t, :], pg[:].indirect(l6[:]), COPY, scale=sd_t[:, t : t + 1])
+
+        scatter(0)
+        pairs = [fetch_stops(0)]
+        for t in range(1, PACK):
+            scatter(t)
+            pairs.append(fetch_stops(t))
+            keep_larger(t - 1, pairs[t - 1])
+        vs_picked = sbuf("vs_picked", [P, N], U16)
+        nc.vector.tensor_copy(vs_picked[:], vs_raw[:].indirect(l7[:]))
+        keep_larger(PACK - 1, pairs[PACK - 1])
+
+        hid_grouped = sbuf("hid_grouped", [P, O, PACK], BF16)
+        nc.vector.tensor_copy(hid_grouped[:], hid[:].rearrange("p t o -> p o t"))
+        hq = sbuf("hq", [P, O], U32)
+        hs = sbuf("hs", [P, O], U8)
+        nc.vector.quantize_mx(out=hq[:].bitcast(FP8X4), scales=hs[:], in_=hid_grouped[:].rearrange("p o t -> p (o t)"))
+
+        for b in range(N // P):
+            y_acc = psum.tile([P, O], F32, name="y_acc%d" % b)
+            nc.tensor.matmul_mx(
+                y_acc[:], lhsT=vs_picked[:, b * P : (b + 1) * P].bitcast(FP4X4), lhsT_scale=vss_picked[:, b * P : (b + 1) * P],
+                rhs=hq[:].bitcast(FP8X4), rhs_scale=hs[:], start=True, stop=True,
+            )
+            y = sbuf("y%d" % b, [P, O], F32)
+            if b == 0:
+                nc.vector.tensor_copy(y[:], y_acc[:])
+                nc.sync.dma_start(out[b * P : (b + 1) * P, :], y[:])
+            else:
+                nc.scalar.copy(y[:], y_acc[:])
+                nc.scalar.dma_start(out[b * P : (b + 1) * P, :], y[:])

@@ -31,7 +31,7 @@ def tile_picked_largercode_plain_one_ladder_store_plain_kernel(
         psum = ctx.enter_context(tc.psum_pool(name="psum", bufs=1))
 
         def sbuf(name, shape, dtype):
-            return keep.tile(shape, dtype, name=name, align_bytes=64)
+            return keep.tile(shape, dtype, name=name, tag=name, align_bytes=64)
 
         def load_list(name, src):
             t = sbuf(name, list(src.shape), U16)
@@ -63,30 +63,27 @@ def tile_picked_largercode_plain_one_ladder_store_plain_kernel(
             return plane
 
         l1 = load_list("l1", offs)
-        ta_rows = [load_rows("ta0", ta, 0)]
         ga_t = load_factor(nc.scalar, "ga_t", ga)
-        gb_t = load_factor(nc.scalar, "gb_t", gb)
         l2 = load_list("l2", offs2)
-        tb_rows = [load_rows("tb0", tb, 0)]
-        ta_rows.append(load_rows("ta1", ta, 1))
-        tb_rows.append(load_rows("tb1", tb, 1))
-        l7 = load_list("l7", offs7)
-        for t in range(2, PACK):
+        gb_t = load_factor(nc.scalar, "gb_t", gb)
+        ta_rows, tb_rows = [], []
+        for t in range(PACK):
             ta_rows.append(load_rows("ta%d" % t, ta, t))
             tb_rows.append(load_rows("tb%d" % t, tb, t))
         w_raw = sbuf("w_raw", [P, R], U32)
         nc.sync.dma_start(w_raw[:].bitcast(I32), w_words[0].rearrange("p n t -> p (n t)").bitcast(I32))
+        l7 = load_list("l7", offs7)
         l3 = load_list("l3", offs3)
         l4 = load_list("l4", offs4)
         l5 = load_list("l5", offs5)
-        sa_t = load_factor(nc.sync, "sa_t", sa)
-        sb_t = load_factor(nc.sync, "sb_t", sb)
+        l6 = load_list("l6", offs6)
         vs_raw = sbuf("vs_raw", [P, Z], U16)
         nc.sync.dma_start(vs_raw[:].bitcast(I32), vs_words[0].bitcast(I32))
-        l6 = load_list("l6", offs6)
-        sd_t = load_factor(nc.sync, "sd_t", sd)
         ws_staged = stage_scales("ws_staged", w_scales)
         vss_staged = stage_scales("vss_staged", vs_scales)
+        sa_t = load_factor(nc.gpsimd, "sa_t", sa)
+        sb_t = load_factor(nc.gpsimd, "sb_t", sb)
+        sd_t = load_factor(nc.gpsimd, "sd_t", sd)
 
         board = [sbuf("board%d" % t, [P, C], F32) for t in range(PACK)]
         for t in range(PACK):
@@ -105,29 +102,36 @@ def tile_picked_largercode_plain_one_ladder_store_plain_kernel(
         xs = sbuf("xs", [P, J], U8)
         halves = [slice(h * HALF, (h + 1) * HALF) for h in range(2)]
         cols = [slice(h * HALF // 16, (h + 1) * HALF // 16) for h in range(2)]
-        for t in range(PACK):
-            pa = sbuf("pa%d" % t, [P, J], F32)
-            pb = [sbuf("pb%d_%d" % (t, h), [P, HALF], F32) for h in range(2)] if t == PACK - 1 else None
-            nc.scalar.activation(pa[:], ta_rows[t][:].indirect(l1[:]), COPY, scale=ga_t[:, t : t + 1])
-            if t < PACK - 1:
-                pbw = sbuf("pb%d" % t, [P, J], F32)
-                nc.scalar.activation(pbw[:], tb_rows[t][:].indirect(l2[:]), COPY, scale=gb_t[:, t : t + 1])
-                for h in range(2):
-                    nc.vector.tensor_tensor(xc[h][:, :, t], pa[:, halves[h]], pbw[:, halves[h]], MAX)
-            else:
-                for h in range(2):
-                    nc.scalar.activation(pb[h][:], tb_rows[t][:].indirect(l2[:, cols[h]]), COPY, scale=gb_t[:, t : t + 1])
-                for h in range(2):
-                    nc.vector.tensor_tensor(xc[h][:, :, t], pa[:, halves[h]], pb[h][:], MAX)
+        for u in range(2):
+            pa = sbuf("pa%d" % u, [P, 2, J], F32)
+            pb = sbuf("pb%d" % u, [P, 2, J], F32)
+            for e in range(2):
+                t = 2 * u + e
+                nc.scalar.activation(pa[:, e, :], ta_rows[t][:].indirect(l1[:]), COPY, scale=ga_t[:, t : t + 1])
+                if t < PACK - 1:
+                    nc.scalar.activation(pb[:, e, :], tb_rows[t][:].indirect(l2[:]), COPY, scale=gb_t[:, t : t + 1])
+                else:
+                    for h in range(2):
+                        nc.scalar.activation(
+                            pb[:, e, halves[h]], tb_rows[t][:].indirect(l2[:, cols[h]]), COPY, scale=gb_t[:, t : t + 1]
+                        )
+            for h in range(2):
+                nc.vector.tensor_tensor(
+                    xc[h][:, :, 2 * u : 2 * u + 2],
+                    pa[:, :, halves[h]].rearrange("p e j -> p j e"),
+                    pb[:, :, halves[h]].rearrange("p e j -> p j e"),
+                    MAX,
+                )
         for h in range(2):
             nc.vector.quantize_mx(
                 out=xq[:, halves[h]].bitcast(FP8X4), scales=xs[:, halves[h]], in_=xc[h][:].rearrange("p j t -> p (j t)")
             )
 
         w_dealt = sbuf("w_dealt", [P, R], U32)
-        nc.scalar.copy(
-            w_dealt[:].rearrange("p (t m) -> p m t", t=PACK), w_raw[:].rearrange("p (m t) -> p m t", t=PACK)
-        )
+        dealt = w_dealt[:].rearrange("p (t m) -> p m t", t=PACK)
+        plain = w_raw[:].rearrange("p (m t) -> p m t", t=PACK)
+        nc.scalar.copy(dealt[:, :, 0], plain[:, :, 0])
+        nc.scalar.copy(dealt[:, :, 1:PACK], plain[:, :, 1:PACK])
 
         def first_product(name, t, js):
             n = js.stop - js.start
@@ -143,7 +147,6 @@ def tile_picked_largercode_plain_one_ladder_store_plain_kernel(
         a0 = [first_product("0_%d" % h, 0, halves[h]) for h in range(2)]
         a_rest = [first_product("%d" % t, t, slice(0, J)) for t in range(1, PACK)]
 
-        hid = sbuf("hid", [P, PACK, O], BF16)
 
         def scatter(t):
             if t == 0:
@@ -164,18 +167,20 @@ def tile_picked_largercode_plain_one_ladder_store_plain_kernel(
             nc.vector.tensor_tensor(pg[:], pair[0][:], pair[1][:], MAX)
             nc.scalar.activation(hid[:, t, :], pg[:].indirect(l6[:]), COPY, scale=sd_t[:, t : t + 1])
 
-        scatter(0)
-        pairs = [fetch_stops(0)]
-        for t in range(1, PACK):
+        for t in range(PACK):
             scatter(t)
-            pairs.append(fetch_stops(t))
-            keep_larger(t - 1, pairs[t - 1])
-        vs_picked = sbuf("vs_picked", [P, N], U16)
-        nc.vector.tensor_copy(vs_picked[:], vs_raw[:].indirect(l7[:]))
-        keep_larger(PACK - 1, pairs[PACK - 1])
-
+        pairs = [fetch_stops(t) for t in range(PACK)]
+        hid = keep.tile([P, PACK, O], BF16, name="hid", tag="sa_t", align_bytes=64)
         hid_grouped = sbuf("hid_grouped", [P, O, PACK], BF16)
-        nc.vector.tensor_copy(hid_grouped[:], hid[:].rearrange("p t o -> p o t"))
+        for t in range(PACK):
+            if t == PACK - 1:
+                vs_picked = keep.tile([P, N], U16, name="vs_picked", tag="a_3", align_bytes=64)
+                nc.vector.tensor_copy(vs_picked[:], vs_raw[:].indirect(l7[:]))
+            keep_larger(t, pairs[t])
+        for u in range(2):
+            nc.vector.tensor_copy(
+                hid_grouped[:, :, 2 * u : 2 * u + 2], hid[:, 2 * u : 2 * u + 2, :].rearrange("p e o -> p o e")
+            )
         hq = sbuf("hq", [P, O], U32)
         hs = sbuf("hs", [P, O], U8)
         nc.vector.quantize_mx(out=hq[:].bitcast(FP8X4), scales=hs[:], in_=hid_grouped[:].rearrange("p o t -> p (o t)"))

@@ -48,18 +48,9 @@ def tile_picked_largercode_plain_one_ladder_store_plain_kernel(
             nc.sync.dma_start(rows[:], src.rearrange("(p t) c -> p t c", t=PACK)[:, t, :])
             return rows
 
-        def stage_scales(name, src):
-            width = src.shape[2]
-            staged = sbuf(name, [4, 4, width // 4], I32)
-            nc.gpsimd.dma_start(staged[:], src[0].rearrange("(q i) c -> i q c", i=4).bitcast(I32))
-            return staged
-
-        def spread_scales(name, staged):
-            words = staged.shape[2]
-            plane = sbuf(name, [P, 4 * words], U8)
+        def zeroed_plane(name, width):
+            plane = sbuf(name, [P, width], U8)
             nc.vector.memset(plane[:].bitcast(I32), 0)
-            for q in range(4):
-                nc.vector.tensor_copy(plane[32 * q : 32 * q + 4, :].bitcast(I32), staged[:, q, :])
             return plane
 
         l1 = load_list("l1", offs)
@@ -72,15 +63,24 @@ def tile_picked_largercode_plain_one_ladder_store_plain_kernel(
             tb_rows.append(load_rows("tb%d" % t, tb, t))
         w_raw = sbuf("w_raw", [P, R], U32)
         nc.sync.dma_start(w_raw[:].bitcast(I32), w_words[0].rearrange("p n t -> p (n t)").bitcast(I32))
-        l7 = load_list("l7", offs7)
         l3 = load_list("l3", offs3)
         l4 = load_list("l4", offs4)
         l5 = load_list("l5", offs5)
         l6 = load_list("l6", offs6)
+        l7 = load_list("l7", offs7)
         vs_raw = sbuf("vs_raw", [P, Z], U16)
         nc.sync.dma_start(vs_raw[:].bitcast(I32), vs_words[0].bitcast(I32))
-        ws_staged = stage_scales("ws_staged", w_scales)
-        vss_staged = stage_scales("vss_staged", vs_scales)
+        vss_plain = zeroed_plane("vss_plain", Z)
+        for q in range(4):
+            nc.sync.dma_start(
+                vss_plain[32 * q : 32 * q + 4, :].bitcast(I32), vs_scales[0, 4 * q : 4 * q + 4, :].bitcast(I32)
+            )
+        ws_staged = sbuf("ws_staged", [P, 2, R // 4], I32)
+        for g in range(2):
+            nc.gpsimd.dma_start(
+                ws_staged[64 * g : 64 * g + 4, :, :],
+                w_scales[0, 8 * g : 8 * g + 8, :].rearrange("(q i) c -> i q c", i=4).bitcast(I32),
+            )
         sa_t = load_factor(nc.gpsimd, "sa_t", sa)
         sb_t = load_factor(nc.gpsimd, "sb_t", sb)
         sd_t = load_factor(nc.gpsimd, "sd_t", sd)
@@ -88,14 +88,14 @@ def tile_picked_largercode_plain_one_ladder_store_plain_kernel(
         board = [sbuf("board%d" % t, [P, C], F32) for t in range(PACK)]
         for t in range(PACK):
             nc.vector.memset(board[t][:], 0.0)
-        ws_plain = spread_scales("ws_plain", ws_staged)
+        ws_plain = zeroed_plane("ws_plain", R)
+        for q in range(4):
+            first = 64 * (q // 2)
+            nc.vector.tensor_copy(ws_plain[32 * q : 32 * q + 4, :].bitcast(I32), ws_staged[first : first + 4, q % 2, :])
         ws_dealt = sbuf("ws_dealt", [P, R], U8)
         nc.vector.tensor_copy(
-            ws_dealt[:].rearrange("p (t m) -> p m t", t=PACK), ws_plain[:].rearrange("p (m t) -> p m t", t=PACK)
+            ws_dealt[:].rearrange("p (t m) -> p t m", t=PACK), ws_plain[:].rearrange("p (m t) -> p t m", t=PACK)
         )
-        vss_plain = spread_scales("vss_plain", vss_staged)
-        vss_picked = sbuf("vss_picked", [P, N], U8)
-        nc.vector.tensor_copy(vss_picked[:], vss_plain[:].indirect(l7[:]))
 
         xc = [sbuf("xc%d" % h, [P, HALF, PACK], BF16) for h in range(2)]
         xq = sbuf("xq", [P, J], U32)
@@ -171,12 +171,14 @@ def tile_picked_largercode_plain_one_ladder_store_plain_kernel(
             scatter(t)
         pairs = [fetch_stops(t) for t in range(PACK)]
         hid = keep.tile([P, PACK, O], BF16, name="hid", tag="sa_t", align_bytes=64)
-        hid_grouped = sbuf("hid_grouped", [P, O, PACK], BF16)
         for t in range(PACK):
             if t == PACK - 1:
                 vs_picked = keep.tile([P, N], U16, name="vs_picked", tag="a_3", align_bytes=64)
                 nc.vector.tensor_copy(vs_picked[:], vs_raw[:].indirect(l7[:]))
             keep_larger(t, pairs[t])
+        vss_picked = keep.tile([P, N], U8, name="vss_picked", tag="own2", align_bytes=64)
+        nc.vector.tensor_copy(vss_picked[:], vss_plain[:].indirect(l7[:]))
+        hid_grouped = keep.tile([P, O, PACK], BF16, name="hid_grouped", tag="vss_plain", align_bytes=64)
         for u in range(2):
             nc.vector.tensor_copy(
                 hid_grouped[:, :, 2 * u : 2 * u + 2], hid[:, 2 * u : 2 * u + 2, :].rearrange("p e o -> p o e")

from contextlib import ExitStack

import concourse.mybir as mybir

K, J, R, T, U, C, O, S, N, Z = 512, 256, 512, 512, 512, 512, 128, 256, 256, 1024
FLOPS = 2 * K * R * J + 2 * R * N * O

F32 = mybir.dt.float32
BF16 = mybir.dt.bfloat16
I32 = mybir.dt.int32
U32 = mybir.dt.uint32
U16 = mybir.dt.uint16
U8 = mybir.dt.uint8
FP8X4 = mybir.dt.float8_e4m3fn_x4
FP4X4 = mybir.dt.float4_e2m1fn_x4
COPY = mybir.ActivationFunctionType.Copy
MAX = mybir.AluOpType.max

P = 128
PACK = 4
HALF = J // 2


def tile_picked_largercode_plain_one_ladder_store_plain_kernel(
    tc, ta, tb, ga, gb, w_words, w_scales, sa, sb, sd, vs_words, vs_scales,
    offs, offs2, offs3, offs4, offs5, offs6, offs7, out,
):
    nc = tc.nc
    with ExitStack() as ctx:
        keep = ctx.enter_context(tc.tile_pool(name="keep", bufs=1))
        psum = ctx.enter_context(tc.psum_pool(name="psum", bufs=1))

        def sbuf(name, shape, dtype):
            return keep.tile(shape, dtype, name=name, tag=name, align_bytes=64)

        def load_list(name, src):
            t = sbuf(name, list(src.shape), U16)
            nc.sync.dma_start(t[:], src)
            return t

        def load_factor(queue, name, src):
            t = sbuf(name, [P, PACK], F32)
            queue.dma_start(t[:], src.rearrange("(p t) o -> p (t o)", t=PACK))
            return t

        def load_rows(name, src, t):
            rows = sbuf(name, [P, src.shape[1]], F32)
            nc.sync.dma_start(rows[:], src.rearrange("(p t) c -> p t c", t=PACK)[:, t, :])
            return rows

        def zeroed_plane(name, width):
            plane = sbuf(name, [P, width], U8)
            nc.vector.memset(plane[:].bitcast(I32), 0)
            return plane

        l1 = load_list("l1", offs)
        ga_t = load_factor(nc.scalar, "ga_t", ga)
        l2 = load_list("l2", offs2)
        gb_t = load_factor(nc.scalar, "gb_t", gb)
        ta_rows, tb_rows = [], []
        for t in range(PACK):
            ta_rows.append(load_rows("ta%d" % t, ta, t))
            tb_rows.append(load_rows("tb%d" % t, tb, t))
        w_raw = sbuf("w_raw", [P, R], U32)
        nc.sync.dma_start(w_raw[:].bitcast(I32), w_words[0].rearrange("p n t -> p (n t)").bitcast(I32))
        l3 = load_list("l3", offs3)
        l4 = load_list("l4", offs4)
        l5 = load_list("l5", offs5)
        l6 = load_list("l6", offs6)
        l7 = load_list("l7", offs7)
        vs_raw = sbuf("vs_raw", [P, Z], U16)
        nc.sync.dma_start(vs_raw[:].bitcast(I32), vs_words[0].bitcast(I32))
        vss_plain = zeroed_plane("vss_plain", Z)
        for q in range(4):
            nc.sync.dma_start(
                vss_plain[32 * q : 32 * q + 4, :].bitcast(I32), vs_scales[0, 4 * q : 4 * q + 4, :].bitcast(I32)
            )
        ws_staged = sbuf("ws_staged", [P, 2, R // 4], I32)
        for g in range(2):
            nc.gpsimd.dma_start(
                ws_staged[64 * g : 64 * g + 4, :, :],
                w_scales[0, 8 * g : 8 * g + 8, :].rearrange("(q i) c -> i q c", i=4).bitcast(I32),
            )
        sa_t = load_factor(nc.gpsimd, "sa_t", sa)
        sb_t = load_factor(nc.gpsimd, "sb_t", sb)
        sd_t = load_factor(nc.gpsimd, "sd_t", sd)

        board = [sbuf("board%d" % t, [P, C], F32) for t in range(PACK)]
        for t in range(PACK):
            nc.vector.memset(board[t][:], 0.0)
        ws_plain = zeroed_plane("ws_plain", R)
        for q in range(4):
            first = 64 * (q // 2)
            nc.vector.tensor_copy(ws_plain[32 * q : 32 * q + 4, :].bitcast(I32), ws_staged[first : first + 4, q % 2, :])
        ws_dealt = sbuf("ws_dealt", [P, R], U8)
        nc.vector.tensor_copy(
            ws_dealt[:].rearrange("p (t m) -> p t m", t=PACK), ws_plain[:].rearrange("p (m t) -> p t m", t=PACK)
        )

        xc = [sbuf("xc%d" % h, [P, HALF, PACK], BF16) for h in range(2)]
        xq = sbuf("xq", [P, J], U32)
        xs = sbuf("xs", [P, J], U8)
        halves = [slice(h * HALF, (h + 1) * HALF) for h in range(2)]
        cols = [slice(h * HALF // 16, (h + 1) * HALF // 16) for h in range(2)]
        for u in range(2):
            pa = sbuf("pa%d" % u, [P, 2, J], F32)
            pb = sbuf("pb%d" % u, [P, 2, J], F32)
            for e in range(2):
                t = 2 * u + e
                nc.scalar.activation(pa[:, e, :], ta_rows[t][:].indirect(l1[:]), COPY, scale=ga_t[:, t : t + 1])
                if t < PACK - 1:
                    nc.scalar.activation(pb[:, e, :], tb_rows[t][:].indirect(l2[:]), COPY, scale=gb_t[:, t : t + 1])
                else:
                    for h in range(2):
                        nc.scalar.activation(
                            pb[:, e, halves[h]], tb_rows[t][:].indirect(l2[:, cols[h]]), COPY, scale=gb_t[:, t : t + 1]
                        )
            for h in range(2):
                nc.vector.tensor_tensor(
                    xc[h][:, :, 2 * u : 2 * u + 2],
                    pa[:, :, halves[h]].rearrange("p e j -> p j e"),
                    pb[:, :, halves[h]].rearrange("p e j -> p j e"),
                    MAX,
                )
        for h in range(2):
            nc.vector.quantize_mx(
                out=xq[:, halves[h]].bitcast(FP8X4), scales=xs[:, halves[h]], in_=xc[h][:].rearrange("p j t -> p (j t)")
            )

        w_dealt = sbuf("w_dealt", [P, R], U32)
        dealt = w_dealt[:].rearrange("p (t m) -> p m t", t=PACK)
        plain = w_raw[:].rearrange("p (m t) -> p m t", t=PACK)
        nc.scalar.copy(dealt[:, :, 0], plain[:, :, 0])
        nc.scalar.copy(dealt[:, :, 1:PACK], plain[:, :, 1:PACK])

        def first_product(name, t, js):
            n = js.stop - js.start
            acc = psum.tile([P, n], F32, name="acc_" + name)
            nc.tensor.matmul_mx(
                acc[:], lhsT=w_dealt[:, t * P : (t + 1) * P].bitcast(FP8X4), lhsT_scale=ws_dealt[:, t * P : (t + 1) * P],
                rhs=xq[:, js].bitcast(FP8X4), rhs_scale=xs[:, js], start=True, stop=True,
            )
            a = sbuf("a_" + name, [P, n], F32)
            nc.scalar.copy(a[:], acc[:])
            return a

        a0 = [first_product("0_%d" % h, 0, halves[h]) for h in range(2)]
        a_rest = [first_product("%d" % t, t, slice(0, J)) for t in range(1, PACK)]


        def scatter(t):
            if t == 0:
                for h in range(2):
                    nc.vector.tensor_copy(board[0][:].indirect(l3[:, cols[h]]), a0[h][:])
            else:
                nc.vector.tensor_copy(board[t][:].indirect(l3[:]), a_rest[t - 1][:])

        def fetch_stops(t):
            own = sbuf("own%d" % t, [P, S], F32)
            shared = sbuf("shared%d" % t, [P, S], F32)
            nc.scalar.activation(own[:], board[t][:].indirect(l4[:]), COPY, scale=sa_t[:, t : t + 1])
            nc.scalar.activation(shared[:], board[t][:].indirect(l5[:]), COPY, scale=sb_t[:, t : t + 1])
            return own, shared

        def keep_larger(t, pair):
            pg = sbuf("pg%d" % t, [P, S], F32)
            nc.vector.tensor_tensor(pg[:], pair[0][:], pair[1][:], MAX)
            nc.scalar.activation(hid[:, t, :], pg[:].indirect(l6[:]), COPY, scale=sd_t[:, t : t + 1])

        for t in range(PACK):
            scatter(t)
        pairs = [fetch_stops(t) for t in range(PACK)]
        hid = keep.tile([P, PACK, O], BF16, name="hid", tag="sa_t", align_bytes=64)
        for t in range(PACK):
            if t == PACK - 1:
                vs_picked = keep.tile([P, N], U16, name="vs_picked", tag="a_3", align_bytes=64)
                nc.vector.tensor_copy(vs_picked[:], vs_raw[:].indirect(l7[:]))
            keep_larger(t, pairs[t])
        vss_picked = keep.tile([P, N], U8, name="vss_picked", tag="own2", align_bytes=64)
        nc.vector.tensor_copy(vss_picked[:], vss_plain[:].indirect(l7[:]))
        hid_grouped = keep.tile([P, O, PACK], BF16, name="hid_grouped", tag="vss_plain", align_bytes=64)
        for u in range(2):
            nc.vector.tensor_copy(
                hid_grouped[:, :, 2 * u : 2 * u + 2], hid[:, 2 * u : 2 * u + 2, :].rearrange("p e o -> p o e")
            )
        hq = sbuf("hq", [P, O], U32)
        hs = sbuf("hs", [P, O], U8)
        nc.vector.quantize_mx(out=hq[:].bitcast(FP8X4), scales=hs[:], in_=hid_grouped[:].rearrange("p o t -> p (o t)"))

        for b in range(N // P):
            y_acc = psum.tile([P, O], F32, name="y_acc%d" % b)
            nc.tensor.matmul_mx(
                y_acc[:], lhsT=vs_picked[:, b * P : (b + 1) * P].bitcast(FP4X4), lhsT_scale=vss_picked[:, b * P : (b + 1) * P],
                rhs=hq[:].bitcast(FP8X4), rhs_scale=hs[:], start=True, stop=True,
            )
            y = sbuf("y%d" % b, [P, O], F32)
            if b == 0:
                nc.vector.tensor_copy(y[:], y_acc[:])
                nc.sync.dma_start(out[b * P : (b + 1) * P, :], y[:])
            else:
                nc.scalar.copy(y[:], y_acc[:])
                nc.scalar.dma_start(out[b * P : (b + 1) * P, :], y[:])
